import numpy as np
import ml_dtypes


def mxq(x, axis, fmt="e4m3"):
    dtype, down = {"e4m3": (ml_dtypes.float8_e4m3fn, 7), "e5m2": (ml_dtypes.float8_e5m2, 14)}[fmt]
    v = np.moveaxis(np.asarray(x, np.float32).astype(ml_dtypes.bfloat16).astype(np.float64), axis, -1)
    blocks = v.reshape(v.shape[:-1] + (-1, 32))
    amax = np.abs(blocks).max(-1, keepdims=True)
    byte = np.maximum(np.where(amax > 0, np.frexp(amax)[1] - 1 + 127, 0) - down, 1)
    scale = np.exp2(byte - 127.0)
    codes = (blocks / scale).astype(np.float32).astype(dtype).astype(np.float64)
    return np.moveaxis((codes * scale).reshape(v.shape), -1, axis)


WIDE = False


def mx_kscale(k):
    if not WIDE:
        return np.ones(k)
    levels = np.array([10, -10, 5, -5, 0])
    if k % 512:
        return np.exp2(np.random.permutation(np.resize(levels, k // 32))).repeat(32)
    a = np.empty((k // 512, 16))
    for p in range(k // 512):
        a[p, :8] = np.random.permutation(np.resize(levels, 8))
        for g in range(8):
            far = levels[np.abs(levels - a[p, g]) >= 10]
            a[p, g + 8] = far[np.random.randint(len(far))]
    return np.exp2(a.ravel()).repeat(32)


def f64(x):
    return np.asarray(x).astype(np.float64)


def striped(idx):
    return np.tile(idx.reshape(-1, 16).T, (8, 1)).astype(np.uint16)


def unstriped(offs):
    return offs[:16].T.reshape(-1).astype(np.int64)


E2M1 = np.array([0.0, 0.5, 1.0, 1.5, 2.0, 3.0, 4.0, 6.0, -0.0, -0.5, -1.0, -1.5, -2.0, -3.0, -4.0, -6.0])


def pack_weight(w, fmt):
    k, n = w.shape
    w = f64(np.asarray(w, np.float32).astype(ml_dtypes.bfloat16)).reshape(k // 32, 32, n)
    amax = np.abs(w).max(1)
    if fmt == "e4m3":
        byte = np.frexp(amax)[1] - 1 + 127 - 7
    else:
        mant, ex = np.frexp(amax / 6.0)
        byte = np.where(mant > 0.5, ex, ex - 1) + 127
    byte = np.clip(np.where(amax > 0, byte, 1), 1, 254)
    scaled = (w * np.exp2(127.0 - byte)[:, None, :]).reshape(k, n).astype(np.float32)
    by_word = np.ascontiguousarray(scaled.reshape(k // 512, 128, 4, n).transpose(0, 1, 3, 2))
    if fmt == "e4m3":
        words = by_word.astype(ml_dtypes.float8_e4m3fn).view(np.uint8)
    else:
        c = by_word.astype(ml_dtypes.float4_e2m1fn).view(np.uint8) & 0xF
        words = (c[..., 0::2] | (c[..., 1::2] << 4)).reshape(k // 512, 128, 2 * n)
    return np.ascontiguousarray(words), np.ascontiguousarray(byte.astype(np.uint8).reshape(k // 512, 16, n))


def unpack_weight(words, scales, fmt):
    g, _, n = scales.shape
    words = np.ascontiguousarray(words).reshape(g, 128, n, -1)
    if fmt == "e4m3":
        vals = words.view(ml_dtypes.float8_e4m3fn).astype(np.float64)
    else:
        nib = np.empty((g, 128, n, 4), np.uint8)
        nib[..., 0::2] = words & 0xF
        nib[..., 1::2] = words >> 4
        vals = E2M1[nib]
    vals = vals * np.repeat(np.exp2(scales.astype(np.float64) - 127.0), 8, axis=1)[..., None]
    return vals.transpose(0, 1, 3, 2).reshape(g * 512, n)


def planes(y):
    n, m = y.shape
    v = y.astype(np.float32).astype(ml_dtypes.bfloat16).astype(np.float64).reshape(n // 32, 32, m)
    top = np.abs(v).max(1)
    byte = np.clip(np.where(top > 0, np.frexp(top)[1] - 1 + 127 - 7, 1), 1, 254)
    codes = (v * np.exp2(127.0 - byte)[:, None, :]).reshape(n, m).astype(np.float32).astype(ml_dtypes.float8_e4m3fn).view(np.uint8)
    words = codes.reshape(n // 512, 128, 4, m).transpose(0, 1, 3, 2)
    return np.ascontiguousarray(words), np.ascontiguousarray(byte.astype(np.uint8).reshape(n // 512, 16, m))


def silu(v):
    return v / (1.0 + np.exp(-np.maximum(v, -700.0)))


K, T, E1, C1, E2, C2, H = 1024, 512, 4, 128, 4, 128, 512
N = 512


def by_expert(wq, xq, E, C):
    return np.concatenate([wq[e].T @ xq[:, e * C:(e + 1) * C] for e in range(E)], axis=1)


def setup_inputs():
    n = np.random.standard_normal
    s = mx_kscale(K)
    u = mx_kscale(H)
    slots1, slots2 = np.random.permutation(T), np.random.permutation(T)
    x = pack_weight(n((K, T)) * s[:, None], "e4m3")
    wa = [pack_weight(m, "e2m1") for m in n((E1, K, H)) / np.sqrt(K) / s[None, :, None]]
    wb = [pack_weight(m, "e2m1") for m in n((E2, K, H)) / np.sqrt(K) / s[None, :, None] * u]
    w2 = pack_weight(n((H, N)) / np.sqrt(H) / u[:, None], "e2m1")
    return {
        "x_words": x[0],
        "x_scales": x[1],
        "wa_words": np.stack([m[0] for m in wa]),
        "wa_scales": np.stack([m[1] for m in wa]),
        "wb_words": np.stack([m[0] for m in wb]),
        "wb_scales": np.stack([m[1] for m in wb]),
        "w2_words": w2[0],
        "w2_scales": w2[1],
        "offs": striped(slots1),
        "offs2": striped(slots2),
    }


def reference(x_words, x_scales, wa_words, wa_scales, wb_words, wb_scales, w2_words, w2_scales, offs, offs2):
    wa = np.stack([unpack_weight(wa_words[e], wa_scales[e], "e2m1") for e in range(E1)])
    wb = np.stack([unpack_weight(wb_words[e], wb_scales[e], "e2m1") for e in range(E2)])
    w2 = unpack_weight(w2_words, w2_scales, "e2m1")
    idx, idx2 = unstriped(offs), unstriped(offs2)
    x = unpack_weight(x_words, x_scales, "e4m3")
    a, c = np.zeros((H, T)), np.zeros((H, T))
    a[:, idx] = by_expert(wa, x[:, idx], E1, C1)
    c[:, idx2] = by_expert(wb, x[:, idx2], E2, C2)
    out_0 = w2.T @ mxq(silu(a) * c, 0, "e4m3")
    return (out_0,) + planes(out_0)

@@ -1,0 +1,211 @@
+from contextlib import ExitStack
+
+import concourse.mybir as mybir
+from concourse.masks import make_identity
+
+K, T, E, C, H, N = 1024, 512, 4, 128, 512, 512
+FLOPS = 2 * (2 * K * H * T + H * N * T)
+
+F32 = mybir.dt.float32
+BF16 = mybir.dt.bfloat16
+I32 = mybir.dt.int32
+U32 = mybir.dt.uint32
+U16 = mybir.dt.uint16
+U8 = mybir.dt.uint8
+FP8X4 = mybir.dt.float8_e4m3fn_x4
+FP4X4 = mybir.dt.float4_e2m1fn_x4
+SILU = mybir.ActivationFunctionType.Silu
+MULT = mybir.AluOpType.mult
+
+P = 128
+PACK = 4
+PASSES = K // (P * PACK)
+HALF = T // 2
+WINDOW = 768
+CHUNK = 128
+BANK = 512
+AL = 64
+
+
+def tile_moe_pool_silu_kernel(
+    tc, x_words, x_scales, wa_words, wa_scales, wb_words, wb_scales, w2_words, w2_scales, offs, offs2,
+    out_0, out_1, out_2,
+):
+    nc = tc.nc
+    with ExitStack() as ctx:
+        keep = ctx.enter_context(tc.tile_pool(name="keep", bufs=1))
+        ring = ctx.enter_context(tc.tile_pool(name="ring", bufs=2))
+        psum = ctx.enter_context(tc.psum_pool(name="psum", bufs=1))
+
+        lists = [keep.tile([P, T // 16], U16, name="list_a"), keep.tile([P, T // 16], U16, name="list_b")]
+        xs = keep.tile([P, PASSES, T], U8, align_bytes=AL)
+        xw = keep.tile([P, PASSES, T], I32, align_bytes=AL)
+        ws = keep.tile([P, E * PASSES, H], U8, align_bytes=AL)
+        w2s = keep.tile([P, N], U8, align_bytes=AL)
+        w2w = keep.tile([P, 2 * N], U8, align_bytes=AL)
+        ident = keep.tile([P, P], F32, align_bytes=AL)
+
+        nc.vector.memset(xs[:].bitcast(I32), 0)
+        nc.vector.memset(ws[:].bitcast(I32), 0)
+        nc.vector.memset(w2s[:].bitcast(I32), 0)
+        make_identity(nc, ident[:])
+
+        def load_scale_rows(plane, rows):
+            for q in range(4):
+                nc.sync.dma_start(out=plane[32 * q : 32 * q + 4].bitcast(I32), in_=rows[4 * q : 4 * q + 4].bitcast(I32))
+
+        def load_words(w_words, pair):
+            ww = ring.tile([P, 2 * PASSES, 2 * H], U8, name="ww", align_bytes=AL)
+            src = w_words[2 * pair : 2 * pair + 2].rearrange("e s p b -> p (e s) b")
+            nc.sync.dma_start(out=ww[:].bitcast(I32), in_=src.bitcast(I32))
+            return ww
+
+        nc.sync.dma_start(lists[0][:], offs)
+        load_scale_rows(xs, x_scales.rearrange("s b t -> b s t"))
+        nc.sync.dma_start(out=xw[:], in_=x_words.rearrange("s p t d -> p s (t d)").bitcast(I32))
+        wa0 = load_words(wa_words, 0)
+        nc.sync.dma_start(lists[1][:], offs2)
+        load_scale_rows(ws, wa_scales.rearrange("e s b i -> b (e s) i"))
+        wa1 = load_words(wa_words, 1)
+        load_scale_rows(w2s, w2_scales[0])
+        nc.sync.dma_start(out=w2w[:].bitcast(I32), in_=w2_words[0].bitcast(I32))
+
+        def gather(pool, half):
+            offsets = lists[pool][:, half * (HALF // 16) : (half + 1) * (HALF // 16)]
+            got = []
+            for s in range(PASSES):
+                gs = keep.tile([P, HALF], U8, name=f"gs{pool}{half}{s}", align_bytes=AL)
+                gw = keep.tile([P, HALF], U32, name=f"gw{pool}{half}{s}", align_bytes=AL)
+                nc.vector.tensor_copy(gs[:], xs[:, s, :].indirect(offsets))
+                nc.vector.tensor_copy(gw[:], xw[:, s, :].bitcast(U32).indirect(offsets))
+                got.append((gw, gs))
+            return got
+
+        gathered = [[gather(pool, half) for half in range(2)] for pool in range(2)]
+
+        w2wp = keep.tile([P, PACK, 2 * P], U8, align_bytes=AL)
+        w2sp = keep.tile([P, PACK, P], U8, align_bytes=AL)
+        nc.vector.tensor_copy(w2wp[:].bitcast(U16), w2w[:].bitcast(U16).rearrange("p (m d) -> p d m", d=PACK))
+        nc.vector.tensor_copy(w2sp[:], w2s[:].rearrange("p (m d) -> p d m", d=PACK))
+
+        windows = [[keep.tile([P, WINDOW], F32, name=f"win{pool}{t}", align_bytes=AL) for t in range(PACK)] for pool in range(2)]
+
+        def expert(pool, half, j, ww):
+            e = 2 * half + j
+            acc = psum.tile([P, BANK], F32, name="acc", bufs=3)
+            for s in range(PASSES):
+                gw, gs = gathered[pool][half][s]
+                nc.tensor.matmul_mx(
+                    out=acc[:],
+                    lhsT=gw[:, j * C : (j + 1) * C].bitcast(FP8X4),
+                    lhsT_scale=gs[:, j * C : (j + 1) * C],
+                    rhs=ww[:, j * PASSES + s, :].bitcast(FP4X4),
+                    rhs_scale=ws[:, e * PASSES + s, :],
+                    start=(s == 0),
+                    stop=(s == PASSES - 1),
+                )
+            by_slot = keep.tile([P, PACK, P], F32, name=f"by_slot{e}", align_bytes=AL)
+            dealt = acc[:].rearrange("u (m t) -> u t m", t=PACK)
+            if pool == 0:
+                nc.scalar.activation(by_slot[:], dealt, SILU)
+            else:
+                nc.scalar.copy(by_slot[:], dealt)
+            return by_slot
+
+        def turn_and_scatter(pool, by_slots, first_slot, planes):
+            width = len(by_slots) * C
+            turned = psum.tile([P, len(planes), width], F32, name="turned", bufs=4)
+            for tt, t in enumerate(planes):
+                for j, by_slot in enumerate(by_slots):
+                    nc.tensor.transpose(turned[:, tt, j * C : (j + 1) * C], by_slot[:, t, :], ident[:])
+            by_feature = keep.tile([P, len(planes), width], F32, name=f"by_feature{pool}{first_slot}{planes[0]}", align_bytes=AL)
+            nc.scalar.copy(by_feature[:], turned[:])
+            offsets = lists[pool][:, first_slot // 16 : (first_slot + width) // 16]
+            for tt, t in enumerate(planes):
+                nc.vector.tensor_copy(windows[pool][t][:].indirect(offsets), by_feature[:, tt, :])
+
+        for half, ww in enumerate((wa0, wa1)):
+            by_slots = [expert(0, half, j, ww) for j in range(2)]
+            for planes in ((0, 1), (2, 3)):
+                turn_and_scatter(0, by_slots, half * HALF, planes)
+
+        load_scale_rows(ws, wb_scales.rearrange("e s b i -> b (e s) i"))
+        by_slots = []
+        for half in range(2):
+            ww = load_words(wb_words, half)
+            by_slots.extend(expert(1, half, j, ww) for j in range(2))
+
+        h_planes = keep.tile([P, PACK, T], BF16, align_bytes=AL)
+
+        def gate(t, cols):
+            nc.vector.tensor_tensor(h_planes[:, t, cols], windows[0][t][:, cols], windows[1][t][:, cols], MULT)
+
+        for t in range(PACK):
+            turn_and_scatter(1, by_slots, 0, (t,))
+            if t < PACK - 1:
+                gate(t, slice(0, T))
+
+        chunks = [slice(c * CHUNK, (c + 1) * CHUNK) for c in range(T // CHUNK)]
+        y_codes = keep.tile([P, T], U32, align_bytes=AL)
+        y_scales = keep.tile([P, T], U8, align_bytes=AL)
+        out_rows = out_0.rearrange("(p d) t -> p d t", d=PACK)
+
+        def group_h(c, copy):
+            grouped = keep.tile([P, CHUNK, PACK], BF16, name=f"h_grouped{c}", align_bytes=AL)
+            copy(
+                grouped[:].rearrange("p (g i) t -> p g t i", i=4),
+                h_planes[:, :, chunks[c]].rearrange("p t (g i) -> p g t i", i=4),
+            )
+            return grouped
+
+        def second_layer(c, grouped):
+            hq = keep.tile([P, CHUNK], U32, name=f"hq{c}", align_bytes=AL)
+            hs = keep.tile([P, CHUNK], U8, name=f"hs{c}", align_bytes=AL)
+            nc.vector.quantize_mx(out=hq[:].bitcast(FP8X4), scales=hs[:], in_=grouped[:].rearrange("p g t -> p (g t)"))
+            acc = psum.tile([P, PACK, CHUNK], F32, name="turned", bufs=4)
+            for d in range(PACK):
+                nc.tensor.matmul_mx(
+                    out=acc[:, d, :],
+                    lhsT=w2wp[:, d, :].bitcast(FP4X4),
+                    lhsT_scale=w2sp[:, d, :],
+                    rhs=hq[:].bitcast(FP8X4),
+                    rhs_scale=hs[:],
+                    start=True,
+                    stop=True,
+                )
+            return acc
+
+        def store_y(c, acc):
+            y = keep.tile([P, PACK, CHUNK], F32, name=f"y{c}", align_bytes=AL)
+            nc.scalar.copy(y[:], acc[:])
+            nc.sync.dma_start(out=out_rows[:, :, chunks[c]], in_=y[:])
+            return y
+
+        def quantise_y(c, source):
+            grouped = keep.tile([P, CHUNK, PACK], BF16, name=f"y_grouped{c}", align_bytes=AL)
+            nc.vector.tensor_copy(
+                grouped[:].rearrange("p (g i) d -> p g d i", i=4), source[:].rearrange("p d (g i) -> p g d i", i=4)
+            )
+            nc.vector.quantize_mx(
+                out=y_codes[:, chunks[c]].bitcast(FP8X4),
+                scales=y_scales[:, chunks[c]],
+                in_=grouped[:].rearrange("p g d -> p (g d)"),
+            )
+
+        gate(PACK - 1, chunks[0])
+        gate(PACK - 1, chunks[1])
+        g0 = group_h(0, nc.vector.tensor_copy)
+        gate(PACK - 1, slice(HALF, T))
+        g1 = group_h(1, nc.scalar.copy)
+        acc0 = second_layer(0, g0)
+        g2 = group_h(2, nc.vector.tensor_copy)
+        g3 = group_h(3, nc.scalar.copy)
+        accs = [acc0, second_layer(1, g1), second_layer(2, g2), second_layer(3, g3)]
+        for c in range(3):
+            quantise_y(c, store_y(c, accs[c]))
+        quantise_y(3, accs[3])
+        store_y(3, accs[3])
+        nc.sync.dma_start(out=out_1[0].rearrange("p t d -> p (t d)").bitcast(I32), in_=y_codes[:].bitcast(I32))
+        for q in range(4):
+            eng = nc.sync if q % 2 else nc.scalar
+            eng.dma_start(out=out_2[0, 4 * q : 4 * q + 4, :].bitcast(I32), in_=y_scales[32 * q : 32 * q + 4, :].bitcast(I32))

@@ -34,20 +34,20 @@ def tile_moe_pool_silu_kernel(
     nc = tc.nc
     with ExitStack() as ctx:
         keep = ctx.enter_context(tc.tile_pool(name="keep", bufs=1))
-        ring = ctx.enter_context(tc.tile_pool(name="ring", bufs=2))
+        ring = ctx.enter_context(tc.tile_pool(name="ring", bufs=1))
         psum = ctx.enter_context(tc.psum_pool(name="psum", bufs=1))
 
         lists = [keep.tile([P, T // 16], U16, name="list_a"), keep.tile([P, T // 16], U16, name="list_b")]
-        xs = keep.tile([P, PASSES, T], U8, align_bytes=AL)
+        xs = keep.tile([P, WINDOW], U8, tag="xs", align_bytes=AL)
+        gs1 = [keep.tile([P, T], U8, name=f"gs1{pool}", align_bytes=AL) for pool in range(2)]
         xw = keep.tile([P, PASSES, T], I32, align_bytes=AL)
         ws = keep.tile([P, E * PASSES, H], U8, align_bytes=AL)
-        w2s = keep.tile([P, N], U8, align_bytes=AL)
-        w2w = keep.tile([P, 2 * N], U8, align_bytes=AL)
         ident = keep.tile([P, P], F32, align_bytes=AL)
 
-        nc.vector.memset(xs[:].bitcast(I32), 0)
+        nc.gpsimd.memset(xs[:].bitcast(I32), 0)
         nc.vector.memset(ws[:].bitcast(I32), 0)
-        nc.vector.memset(w2s[:].bitcast(I32), 0)
+        for plane in gs1:
+            nc.vector.memset(plane[:].bitcast(I32), 0)
         make_identity(nc, ident[:])
 
         def load_scale_rows(plane, rows):
@@ -61,32 +61,39 @@ def tile_moe_pool_silu_kernel(
             return ww
 
         nc.sync.dma_start(lists[0][:], offs)
-        load_scale_rows(xs, x_scales.rearrange("s b t -> b s t"))
+        nc.sync.dma_start(lists[1][:], offs2)
+        for q in range(4):
+            nc.scalar.dma_start(
+                out=xs[32 * q : 32 * q + 8, 0:T].bitcast(I32), in_=x_scales[:, 4 * q : 4 * q + 4, :].bitcast(I32)
+            )
         nc.sync.dma_start(out=xw[:], in_=x_words.rearrange("s p t d -> p s (t d)").bitcast(I32))
         wa0 = load_words(wa_words, 0)
-        nc.sync.dma_start(lists[1][:], offs2)
         load_scale_rows(ws, wa_scales.rearrange("e s b i -> b (e s) i"))
-        wa1 = load_words(wa_words, 1)
-        load_scale_rows(w2s, w2_scales[0])
-        nc.sync.dma_start(out=w2w[:].bitcast(I32), in_=w2_words[0].bitcast(I32))
 
-        def gather(pool, half):
+        def gather_scales(pool):
+            gs = keep.tile([P, T], U8, name=f"gs{pool}", align_bytes=AL)
+            nc.vector.tensor_copy(gs[:], xs[:].indirect(lists[pool][:]))
+            queue = nc.sync
+            for q in range(4):
+                queue.dma_start(
+                    out=gs1[pool][32 * q : 32 * q + 4, :].bitcast(I32), in_=gs[32 * q + 4 : 32 * q + 8, :].bitcast(I32)
+                )
+            return gs, gs1[pool]
+
+        def gather_words(pool, half, gw):
             offsets = lists[pool][:, half * (HALF // 16) : (half + 1) * (HALF // 16)]
-            got = []
             for s in range(PASSES):
-                gs = keep.tile([P, HALF], U8, name=f"gs{pool}{half}{s}", align_bytes=AL)
-                gw = keep.tile([P, HALF], U32, name=f"gw{pool}{half}{s}", align_bytes=AL)
-                nc.vector.tensor_copy(gs[:], xs[:, s, :].indirect(offsets))
-                nc.vector.tensor_copy(gw[:], xw[:, s, :].bitcast(U32).indirect(offsets))
-                got.append((gw, gs))
-            return got
+                nc.vector.tensor_copy(gw[:, s * HALF : (s + 1) * HALF], xw[:, s, :].bitcast(U32).indirect(offsets))
+            return [gw[:, s * HALF : (s + 1) * HALF] for s in range(PASSES)]
 
-        gathered = [[gather(pool, half) for half in range(2)] for pool in range(2)]
-
-        w2wp = keep.tile([P, PACK, 2 * P], U8, align_bytes=AL)
-        w2sp = keep.tile([P, PACK, P], U8, align_bytes=AL)
-        nc.vector.tensor_copy(w2wp[:].bitcast(U16), w2w[:].bitcast(U16).rearrange("p (m d) -> p d m", d=PACK))
-        nc.vector.tensor_copy(w2sp[:], w2s[:].rearrange("p (m d) -> p d m", d=PACK))
+        first_words = keep.tile([P, PASSES * HALF], U32, align_bytes=AL)
+        first = gather_words(0, 0, first_words)
+        slot_scales = [gather_scales(pool) for pool in range(2)]
+        later_words = keep.tile([P, 3, PASSES * HALF], U32, tag="xs", align_bytes=AL)
+        gathered = [
+            [first, gather_words(0, 1, later_words[:, 0, :])],
+            [gather_words(1, half, later_words[:, 1 + half, :]) for half in range(2)],
+        ]
 
         windows = [[keep.tile([P, WINDOW], F32, name=f"win{pool}{t}", align_bytes=AL) for t in range(PACK)] for pool in range(2)]
 
@@ -94,11 +101,11 @@ def tile_moe_pool_silu_kernel(
             e = 2 * half + j
             acc = psum.tile([P, BANK], F32, name="acc", bufs=3)
             for s in range(PASSES):
-                gw, gs = gathered[pool][half][s]
+                gw, gs = gathered[pool][half][s], slot_scales[pool][s]
                 nc.tensor.matmul_mx(
                     out=acc[:],
                     lhsT=gw[:, j * C : (j + 1) * C].bitcast(FP8X4),
-                    lhsT_scale=gs[:, j * C : (j + 1) * C],
+                    lhsT_scale=gs[:, e * C : (e + 1) * C],
                     rhs=ww[:, j * PASSES + s, :].bitcast(FP4X4),
                     rhs_scale=ws[:, e * PASSES + s, :],
                     start=(s == 0),
@@ -124,39 +131,54 @@ def tile_moe_pool_silu_kernel(
             for tt, t in enumerate(planes):
                 nc.vector.tensor_copy(windows[pool][t][:].indirect(offsets), by_feature[:, tt, :])
 
-        for half, ww in enumerate((wa0, wa1)):
-            by_slots = [expert(0, half, j, ww) for j in range(2)]
-            for planes in ((0, 1), (2, 3)):
-                turn_and_scatter(0, by_slots, half * HALF, planes)
+        for j in range(2):
+            turn_and_scatter(0, [expert(0, 0, j, wa0)], j * C, (0, 1, 2, 3))
+        ww = load_words(wa_words, 1)
+        by_slots = [expert(0, 1, j, ww) for j in range(2)]
+        for planes in ((0, 1), (2, 3)):
+            turn_and_scatter(0, by_slots, HALF, planes)
 
         load_scale_rows(ws, wb_scales.rearrange("e s b i -> b (e s) i"))
-        by_slots = []
-        for half in range(2):
-            ww = load_words(wb_words, half)
-            by_slots.extend(expert(1, half, j, ww) for j in range(2))
+        ww = load_words(wb_words, 0)
+        by_slots = [expert(1, 0, j, ww) for j in range(2)]
+        for planes in ((0, 1), (2, 3)):
+            turn_and_scatter(1, by_slots, 0, planes)
+        ww = load_words(wb_words, 1)
+        by_slots = [expert(1, 1, j, ww) for j in range(2)]
+
+        w2w = ring.tile([P, 2 * N], U8, name="ww", align_bytes=AL)
+        nc.sync.dma_start(out=w2w[:].bitcast(I32), in_=w2_words[0].bitcast(I32))
+        w2s = ws[:, 0, :]
+        load_scale_rows(w2s, w2_scales[0])
+        w2wp = keep.tile([P, PACK, 2 * P], U8, align_bytes=AL)
+        w2sp = keep.tile([P, PACK, P], U8, align_bytes=AL)
+        nc.vector.tensor_copy(w2wp[:].bitcast(U16), w2w[:].bitcast(U16).rearrange("p (m d) -> p d m", d=PACK))
+        nc.vector.tensor_copy(w2sp[:], w2s.rearrange("p (m d) -> p d m", d=PACK))
 
         h_planes = keep.tile([P, PACK, T], BF16, align_bytes=AL)
 
         def gate(t, cols):
             nc.vector.tensor_tensor(h_planes[:, t, cols], windows[0][t][:, cols], windows[1][t][:, cols], MULT)
 
-        for t in range(PACK):
-            turn_and_scatter(1, by_slots, 0, (t,))
-            if t < PACK - 1:
-                gate(t, slice(0, T))
-
         chunks = [slice(c * CHUNK, (c + 1) * CHUNK) for c in range(T // CHUNK)]
+        h_grouped = [keep.tile([P, CHUNK, PACK], BF16, name=f"h_grouped{c}", align_bytes=AL) for c in range(len(chunks))]
+
+        def group_h(c, first, copy):
+            copy(h_grouped[c][:, :, first : first + 2], h_planes[:, first : first + 2, chunks[c]].rearrange("p t g -> p g t"))
+            return h_grouped[c]
+
+        turn_and_scatter(1, by_slots, HALF, (0, 1))
+        gate(0, slice(0, T))
+        turn_and_scatter(1, by_slots, HALF, (2,))
+        gate(1, slice(0, T))
+        gate(2, slice(0, T))
+        for c in range(len(chunks)):
+            group_h(c, 0, nc.scalar.copy)
+        turn_and_scatter(1, by_slots, HALF, (3,))
+
         y_codes = keep.tile([P, T], U32, align_bytes=AL)
         y_scales = keep.tile([P, T], U8, align_bytes=AL)
         out_rows = out_0.rearrange("(p d) t -> p d t", d=PACK)
-
-        def group_h(c, copy):
-            grouped = keep.tile([P, CHUNK, PACK], BF16, name=f"h_grouped{c}", align_bytes=AL)
-            copy(
-                grouped[:].rearrange("p (g i) t -> p g t i", i=4),
-                h_planes[:, :, chunks[c]].rearrange("p t (g i) -> p g t i", i=4),
-            )
-            return grouped
 
         def second_layer(c, grouped):
             hq = keep.tile([P, CHUNK], U32, name=f"hq{c}", align_bytes=AL)
@@ -194,12 +216,12 @@ def tile_moe_pool_silu_kernel(
 
         gate(PACK - 1, chunks[0])
         gate(PACK - 1, chunks[1])
-        g0 = group_h(0, nc.vector.tensor_copy)
+        g0 = group_h(0, 2, nc.vector.tensor_copy)
         gate(PACK - 1, slice(HALF, T))
-        g1 = group_h(1, nc.scalar.copy)
+        g1 = group_h(1, 2, nc.scalar.copy)
         acc0 = second_layer(0, g0)
-        g2 = group_h(2, nc.vector.tensor_copy)
-        g3 = group_h(3, nc.scalar.copy)
+        g2 = group_h(2, 2, nc.vector.tensor_copy)
+        g3 = group_h(3, 2, nc.scalar.copy)
         accs = [acc0, second_layer(1, g1), second_layer(2, g2), second_layer(3, g3)]
         for c in range(3):
             quantise_y(c, store_y(c, accs[c]))

@@ -41,7 +41,7 @@ def tile_moe_pool_silu_kernel(
         xs = keep.tile([P, WINDOW], U8, tag="xs", align_bytes=AL)
         gs1 = [keep.tile([P, T], U8, name=f"gs1{pool}", align_bytes=AL) for pool in range(2)]
         xw = keep.tile([P, PASSES, T], I32, align_bytes=AL)
-        ws = keep.tile([P, E * PASSES, H], U8, align_bytes=AL)
+        ws = keep.tile([P, 2 * PASSES, H], U8, align_bytes=AL)
         ident = keep.tile([P, P], F32, align_bytes=AL)
 
         nc.gpsimd.memset(xs[:].bitcast(I32), 0)
@@ -54,10 +54,11 @@ def tile_moe_pool_silu_kernel(
             for q in range(4):
                 nc.sync.dma_start(out=plane[32 * q : 32 * q + 4].bitcast(I32), in_=rows[4 * q : 4 * q + 4].bitcast(I32))
 
-        def load_words(w_words, pair):
+        def load_pair(w_words, w_scales, pair):
             ww = ring.tile([P, 2 * PASSES, 2 * H], U8, name="ww", align_bytes=AL)
             src = w_words[2 * pair : 2 * pair + 2].rearrange("e s p b -> p (e s) b")
             nc.sync.dma_start(out=ww[:].bitcast(I32), in_=src.bitcast(I32))
+            load_scale_rows(ws, w_scales[2 * pair : 2 * pair + 2].rearrange("e s b i -> b (e s) i"))
             return ww
 
         nc.sync.dma_start(lists[0][:], offs)
@@ -67,8 +68,7 @@ def tile_moe_pool_silu_kernel(
                 out=xs[32 * q : 32 * q + 8, 0:T].bitcast(I32), in_=x_scales[:, 4 * q : 4 * q + 4, :].bitcast(I32)
             )
         nc.sync.dma_start(out=xw[:], in_=x_words.rearrange("s p t d -> p s (t d)").bitcast(I32))
-        wa0 = load_words(wa_words, 0)
-        load_scale_rows(ws, wa_scales.rearrange("e s b i -> b (e s) i"))
+        wa0 = load_pair(wa_words, wa_scales, 0)
 
         def gather_scales(pool):
             gs = keep.tile([P, T], U8, name=f"gs{pool}", align_bytes=AL)
@@ -107,7 +107,7 @@ def tile_moe_pool_silu_kernel(
                     lhsT=gw[:, j * C : (j + 1) * C].bitcast(FP8X4),
                     lhsT_scale=gs[:, e * C : (e + 1) * C],
                     rhs=ww[:, j * PASSES + s, :].bitcast(FP4X4),
-                    rhs_scale=ws[:, e * PASSES + s, :],
+                    rhs_scale=ws[:, j * PASSES + s, :],
                     start=(s == 0),
                     stop=(s == PASSES - 1),
                 )
@@ -133,17 +133,16 @@ def tile_moe_pool_silu_kernel(
 
         for j in range(2):
             turn_and_scatter(0, [expert(0, 0, j, wa0)], j * C, (0, 1, 2, 3))
-        ww = load_words(wa_words, 1)
+        ww = load_pair(wa_words, wa_scales, 1)
         by_slots = [expert(0, 1, j, ww) for j in range(2)]
         for planes in ((0, 1), (2, 3)):
             turn_and_scatter(0, by_slots, HALF, planes)
 
-        load_scale_rows(ws, wb_scales.rearrange("e s b i -> b (e s) i"))
-        ww = load_words(wb_words, 0)
+        ww = load_pair(wb_words, wb_scales, 0)
         by_slots = [expert(1, 0, j, ww) for j in range(2)]
         for planes in ((0, 1), (2, 3)):
             turn_and_scatter(1, by_slots, 0, planes)
-        ww = load_words(wb_words, 1)
+        ww = load_pair(wb_words, wb_scales, 1)
         by_slots = [expert(1, 1, j, ww) for j in range(2)]
 
         w2w = ring.tile([P, 2 * N], U8, name="ww", align_bytes=AL)
@@ -158,7 +157,8 @@ def tile_moe_pool_silu_kernel(
         h_planes = keep.tile([P, PACK, T], BF16, align_bytes=AL)
 
         def gate(t, cols):
-            nc.vector.tensor_tensor(h_planes[:, t, cols], windows[0][t][:, cols], windows[1][t][:, cols], MULT)
+            engine = nc.vector if t == PACK - 1 else nc.gpsimd
+            engine.tensor_tensor(h_planes[:, t, cols], windows[0][t][:, cols], windows[1][t][:, cols], MULT)
 
         chunks = [slice(c * CHUNK, (c + 1) * CHUNK) for c in range(T // CHUNK)]
         h_grouped = [keep.tile([P, CHUNK, PACK], BF16, name=f"h_grouped{c}", align_bytes=AL) for c in range(len(chunks))]

@@ -3,7 +3,7 @@ from contextlib import ExitStack
 import concourse.mybir as mybir
 from concourse.masks import make_identity
 
-K, T, E, C, H, N = 1024, 512, 4, 128, 512, 512
+K, T, C, H, N = 1024, 512, 128, 512, 512
 FLOPS = 2 * (2 * K * H * T + H * N * T)
 
 F32 = mybir.dt.float32
@@ -19,12 +19,15 @@ MULT = mybir.AluOpType.mult
 
 P = 128
 PACK = 4
+QUADRANTS = 4
 PASSES = K // (P * PACK)
 HALF = T // 2
 WINDOW = 768
 CHUNK = 128
 BANK = 512
-AL = 64
+ALIGN = 64
+SUM_BANKS, TURN_BANKS = 3, 4
+WARM_PASSES = 4
 
 
 def tile_moe_pool_silu_kernel(
@@ -38,196 +41,226 @@ def tile_moe_pool_silu_kernel(
         psum = ctx.enter_context(tc.psum_pool(name="psum", bufs=1))
 
         lists = [keep.tile([P, T // 16], U16, name="list_a"), keep.tile([P, T // 16], U16, name="list_b")]
-        xs = keep.tile([P, WINDOW], U8, tag="xs", align_bytes=AL)
-        gs1 = [keep.tile([P, T], U8, name=f"gs1{pool}", align_bytes=AL) for pool in range(2)]
-        xw = keep.tile([P, PASSES, T], I32, align_bytes=AL)
-        ws = keep.tile([P, 2 * PASSES, H], U8, align_bytes=AL)
-        ident = keep.tile([P, P], F32, align_bytes=AL)
+        x_scale_rows = keep.tile([P, WINDOW], U8, tag="x_scale_rows", align_bytes=ALIGN)
+        second_pass_scales = [keep.tile([P, T], U8, name=f"second_pass_scales{pool}", align_bytes=ALIGN) for pool in range(2)]
+        x_word_rows = keep.tile([P, PASSES, T], I32, align_bytes=ALIGN)
+        pair_scales = keep.tile([P, 2 * PASSES, H], U8, align_bytes=ALIGN)
+        identity = keep.tile([P, P], F32, align_bytes=ALIGN)
 
-        nc.gpsimd.memset(xs[:].bitcast(I32), 0)
-        nc.vector.memset(ws[:].bitcast(I32), 0)
-        for plane in gs1:
-            nc.vector.memset(plane[:].bitcast(I32), 0)
-        make_identity(nc, ident[:])
+        nc.gpsimd.memset(x_scale_rows[:].bitcast(I32), 0)
+        nc.vector.memset(pair_scales[:].bitcast(I32), 0)
+        for scales in second_pass_scales:
+            nc.vector.memset(scales[:].bitcast(I32), 0)
+        make_identity(nc, identity[:])
 
-        def load_scale_rows(plane, rows):
-            for q in range(4):
-                nc.sync.dma_start(out=plane[32 * q : 32 * q + 4].bitcast(I32), in_=rows[4 * q : 4 * q + 4].bitcast(I32))
+        def load_scale_rows(scales, rows):
+            for q in range(QUADRANTS):
+                nc.sync.dma_start(out=scales[32 * q : 32 * q + 4].bitcast(I32), in_=rows[4 * q : 4 * q + 4].bitcast(I32))
 
         def load_pair(w_words, w_scales, pair):
-            ww = ring.tile([P, 2 * PASSES, 2 * H], U8, name="ww", align_bytes=AL)
-            src = w_words[2 * pair : 2 * pair + 2].rearrange("e s p b -> p (e s) b")
-            nc.sync.dma_start(out=ww[:].bitcast(I32), in_=src.bitcast(I32))
-            load_scale_rows(ws, w_scales[2 * pair : 2 * pair + 2].rearrange("e s b i -> b (e s) i"))
-            return ww
+            pair_words = ring.tile([P, 2 * PASSES, 2 * H], U8, align_bytes=ALIGN)
+            source = w_words[2 * pair : 2 * pair + 2].rearrange("e s p b -> p (e s) b")
+            nc.sync.dma_start(out=pair_words[:].bitcast(I32), in_=source.bitcast(I32))
+            load_scale_rows(pair_scales, w_scales[2 * pair : 2 * pair + 2].rearrange("e s b i -> b (e s) i"))
+            return pair_words
 
         nc.sync.dma_start(lists[0][:], offs)
         nc.sync.dma_start(lists[1][:], offs2)
-        for q in range(4):
+        for q in range(QUADRANTS):
             nc.scalar.dma_start(
-                out=xs[32 * q : 32 * q + 8, 0:T].bitcast(I32), in_=x_scales[:, 4 * q : 4 * q + 4, :].bitcast(I32)
+                out=x_scale_rows[32 * q : 32 * q + 8, 0:T].bitcast(I32), in_=x_scales[:, 4 * q : 4 * q + 4, :].bitcast(I32)
             )
-        nc.sync.dma_start(out=xw[:], in_=x_words.rearrange("s p t d -> p s (t d)").bitcast(I32))
-        wa0 = load_pair(wa_words, wa_scales, 0)
+        nc.sync.dma_start(out=x_word_rows[:], in_=x_words.rearrange("s p t d -> p s (t d)").bitcast(I32))
+        pair_words = load_pair(wa_words, wa_scales, 0)
 
         def gather_scales(pool):
-            gs = keep.tile([P, T], U8, name=f"gs{pool}", align_bytes=AL)
-            nc.vector.tensor_copy(gs[:], xs[:].indirect(lists[pool][:]))
-            queue = nc.sync
-            for q in range(4):
-                queue.dma_start(
-                    out=gs1[pool][32 * q : 32 * q + 4, :].bitcast(I32), in_=gs[32 * q + 4 : 32 * q + 8, :].bitcast(I32)
+            both = keep.tile([P, T], U8, name=f"slot_scales{pool}", align_bytes=ALIGN)
+            nc.vector.tensor_copy(both[:], x_scale_rows[:].indirect(lists[pool][:]))
+            for q in range(QUADRANTS):
+                nc.sync.dma_start(
+                    out=second_pass_scales[pool][32 * q : 32 * q + 4, :].bitcast(I32),
+                    in_=both[32 * q + 4 : 32 * q + 8, :].bitcast(I32),
                 )
-            return gs, gs1[pool]
+            return both, second_pass_scales[pool]
 
-        def gather_words(pool, half, gw):
-            offsets = lists[pool][:, half * (HALF // 16) : (half + 1) * (HALF // 16)]
+        def gather_words(pool, pair, targets):
+            offsets = lists[pool][:, pair * (HALF // 16) : (pair + 1) * (HALF // 16)]
             for s in range(PASSES):
-                nc.vector.tensor_copy(gw[:, s * HALF : (s + 1) * HALF], xw[:, s, :].bitcast(U32).indirect(offsets))
-            return [gw[:, s * HALF : (s + 1) * HALF] for s in range(PASSES)]
+                nc.vector.tensor_copy(targets[s], x_word_rows[:, s, :].bitcast(U32).indirect(offsets))
+            return targets
 
-        first_words = keep.tile([P, PASSES * HALF], U32, align_bytes=AL)
-        first = gather_words(0, 0, first_words)
+        first_words = [keep.tile([P, HALF], U32, name=f"first_words{s}", align_bytes=ALIGN) for s in range(PASSES)]
+        first_pair = gather_words(0, 0, [tile[:] for tile in first_words])
         slot_scales = [gather_scales(pool) for pool in range(2)]
-        later_words = keep.tile([P, 3, PASSES * HALF], U32, tag="xs", align_bytes=AL)
-        gathered = [
-            [first, gather_words(0, 1, later_words[:, 0, :])],
-            [gather_words(1, half, later_words[:, 1 + half, :]) for half in range(2)],
+        later_words = keep.tile([P, 3 * PASSES * HALF], U32, tag="x_scale_rows", align_bytes=ALIGN)
+        later = [later_words[:, n * HALF : (n + 1) * HALF] for n in range(3 * PASSES)]
+        slot_words = [
+            [first_pair, gather_words(0, 1, later[0:PASSES])],
+            [gather_words(1, 0, later[PASSES : 2 * PASSES]), gather_words(1, 1, later[2 * PASSES :])],
         ]
 
-        windows = [[keep.tile([P, WINDOW], F32, name=f"win{pool}{t}", align_bytes=AL) for t in range(PACK)] for pool in range(2)]
+        windows = [
+            [keep.tile([P, WINDOW], F32, name=f"window{pool}{t}", align_bytes=ALIGN) for t in range(PACK)] for pool in range(2)
+        ]
 
-        def expert(pool, half, j, ww):
-            e = 2 * half + j
-            acc = psum.tile([P, BANK], F32, name="acc", bufs=3)
+        def expert(pool, pair, j, words):
+            e = 2 * pair + j
+            sums = psum.tile([P, BANK], F32, bufs=SUM_BANKS)
             for s in range(PASSES):
-                gw, gs = gathered[pool][half][s], slot_scales[pool][s]
                 nc.tensor.matmul_mx(
-                    out=acc[:],
-                    lhsT=gw[:, j * C : (j + 1) * C].bitcast(FP8X4),
-                    lhsT_scale=gs[:, e * C : (e + 1) * C],
-                    rhs=ww[:, j * PASSES + s, :].bitcast(FP4X4),
-                    rhs_scale=ws[:, j * PASSES + s, :],
+                    out=sums[:],
+                    lhsT=slot_words[pool][pair][s][:, j * C : (j + 1) * C].bitcast(FP8X4),
+                    lhsT_scale=slot_scales[pool][s][:, e * C : (e + 1) * C],
+                    rhs=words[:, j * PASSES + s, :].bitcast(FP4X4),
+                    rhs_scale=pair_scales[:, j * PASSES + s, :],
                     start=(s == 0),
                     stop=(s == PASSES - 1),
                 )
-            by_slot = keep.tile([P, PACK, P], F32, name=f"by_slot{e}", align_bytes=AL)
-            dealt = acc[:].rearrange("u (m t) -> u t m", t=PACK)
+            by_slot = keep.tile([P, PACK, P], F32, name=f"by_slot{e}", align_bytes=ALIGN)
+            by_plane = sums[:].rearrange("u (p t) -> u t p", t=PACK)
             if pool == 0:
-                nc.scalar.activation(by_slot[:], dealt, SILU)
+                nc.scalar.activation(by_slot[:], by_plane, SILU)
             else:
-                nc.scalar.copy(by_slot[:], dealt)
+                nc.scalar.copy(by_slot[:], by_plane)
             return by_slot
 
         def turn_and_scatter(pool, by_slots, first_slot, planes):
             width = len(by_slots) * C
-            turned = psum.tile([P, len(planes), width], F32, name="turned", bufs=4)
-            for tt, t in enumerate(planes):
+            turned = psum.tile([P, len(planes), width], F32, tag="turned", bufs=TURN_BANKS)
+            for n, t in enumerate(planes):
                 for j, by_slot in enumerate(by_slots):
-                    nc.tensor.transpose(turned[:, tt, j * C : (j + 1) * C], by_slot[:, t, :], ident[:])
-            by_feature = keep.tile([P, len(planes), width], F32, name=f"by_feature{pool}{first_slot}{planes[0]}", align_bytes=AL)
-            nc.scalar.copy(by_feature[:], turned[:])
+                    nc.tensor.transpose(turned[:, n, j * C : (j + 1) * C], by_slot[:, t, :], identity[:])
+            in_slot_order = keep.tile(
+                [P, len(planes), width], F32, name=f"in_slot_order{pool}_{first_slot}_{planes[0]}", align_bytes=ALIGN
+            )
+            nc.scalar.copy(in_slot_order[:], turned[:])
             offsets = lists[pool][:, first_slot // 16 : (first_slot + width) // 16]
-            for tt, t in enumerate(planes):
-                nc.vector.tensor_copy(windows[pool][t][:].indirect(offsets), by_feature[:, tt, :])
+            for n, t in enumerate(planes):
+                nc.vector.tensor_copy(windows[pool][t][:].indirect(offsets), in_slot_order[:, n, :])
 
         for j in range(2):
-            turn_and_scatter(0, [expert(0, 0, j, wa0)], j * C, (0, 1, 2, 3))
-        ww = load_pair(wa_words, wa_scales, 1)
-        by_slots = [expert(0, 1, j, ww) for j in range(2)]
+            turn_and_scatter(0, [expert(0, 0, j, pair_words)], j * C, (0, 1, 2, 3))
+        pair_words = load_pair(wa_words, wa_scales, 1)
+        by_slots = [expert(0, 1, j, pair_words) for j in range(2)]
         for planes in ((0, 1), (2, 3)):
             turn_and_scatter(0, by_slots, HALF, planes)
 
-        ww = load_pair(wb_words, wb_scales, 0)
-        by_slots = [expert(1, 0, j, ww) for j in range(2)]
-        for planes in ((0, 1), (2, 3)):
-            turn_and_scatter(1, by_slots, 0, planes)
-        ww = load_pair(wb_words, wb_scales, 1)
-        by_slots = [expert(1, 1, j, ww) for j in range(2)]
+        w2_raw_words = keep.tile([P, 2 * N], U8, tag="first_words0", align_bytes=ALIGN)
+        nc.sync.dma_start(out=w2_raw_words[:].bitcast(I32), in_=w2_words[0].bitcast(I32))
+        w2_raw_scales = keep.tile([P, N], U8, tag="first_words1", align_bytes=ALIGN)
+        nc.gpsimd.memset(w2_raw_scales[:].bitcast(I32), 0)
+        load_scale_rows(w2_raw_scales, w2_scales[0])
+        w2_plane_words = keep.tile([P, PACK, 2 * P], U8, align_bytes=ALIGN)
+        nc.gpsimd.tensor_copy(
+            w2_plane_words[:].rearrange("p d (m b) -> p d m b", b=2),
+            w2_raw_words[:].rearrange("p (m d b) -> p d m b", d=PACK, b=2),
+        )
+        w2_scales_by_plane = w2_raw_scales[:].rearrange("p (m d) -> p d m", d=PACK)
+        early_scales = keep.tile([P, PACK - 1, P], U8, align_bytes=ALIGN)
+        nc.gpsimd.tensor_copy(early_scales[:], w2_scales_by_plane[:, 0 : PACK - 1, :])
+        w2_plane_scales = [early_scales[:, d, :] for d in range(PACK - 1)]
 
-        w2w = ring.tile([P, 2 * N], U8, name="ww", align_bytes=AL)
-        nc.sync.dma_start(out=w2w[:].bitcast(I32), in_=w2_words[0].bitcast(I32))
-        w2s = ws[:, 0, :]
-        load_scale_rows(w2s, w2_scales[0])
-        w2wp = keep.tile([P, PACK, 2 * P], U8, align_bytes=AL)
-        w2sp = keep.tile([P, PACK, P], U8, align_bytes=AL)
-        nc.vector.tensor_copy(w2wp[:].bitcast(U16), w2w[:].bitcast(U16).rearrange("p (m d) -> p d m", d=PACK))
-        nc.vector.tensor_copy(w2sp[:], w2s.rearrange("p (m d) -> p d m", d=PACK))
+        pair_words = load_pair(wb_words, wb_scales, 0)
+        by_slots_first = [expert(1, 0, j, pair_words) for j in range(2)]
+        for planes in ((0, 1), (2,)):
+            turn_and_scatter(1, by_slots_first, 0, planes)
+        pair_words = load_pair(wb_words, wb_scales, 1)
+        by_slots = [expert(1, 1, j, pair_words) for j in range(2)]
 
-        h_planes = keep.tile([P, PACK, T], BF16, align_bytes=AL)
+        h_planes = keep.tile([P, PACK, T], BF16, align_bytes=ALIGN)
+        chunks = [slice(c * CHUNK, (c + 1) * CHUNK) for c in range(T // CHUNK)]
+        h_grouped = [keep.tile([P, CHUNK, PACK], BF16, name=f"h_grouped{c}", align_bytes=ALIGN) for c in range(len(chunks))]
 
-        def gate(t, cols):
-            engine = nc.vector if t == PACK - 1 else nc.gpsimd
+        def gate(engine, t, cols):
             engine.tensor_tensor(h_planes[:, t, cols], windows[0][t][:, cols], windows[1][t][:, cols], MULT)
 
-        chunks = [slice(c * CHUNK, (c + 1) * CHUNK) for c in range(T // CHUNK)]
-        h_grouped = [keep.tile([P, CHUNK, PACK], BF16, name=f"h_grouped{c}", align_bytes=AL) for c in range(len(chunks))]
-
-        def group_h(c, first, copy):
-            copy(h_grouped[c][:, :, first : first + 2], h_planes[:, first : first + 2, chunks[c]].rearrange("p t g -> p g t"))
-            return h_grouped[c]
+        def group_h(c, first_plane, copy):
+            two = slice(first_plane, first_plane + 2)
+            copy(h_grouped[c][:, :, two], h_planes[:, two, chunks[c]].rearrange("p t g -> p g t"))
 
         turn_and_scatter(1, by_slots, HALF, (0, 1))
-        gate(0, slice(0, T))
+        gate(nc.gpsimd, 0, slice(0, T))
         turn_and_scatter(1, by_slots, HALF, (2,))
-        gate(1, slice(0, T))
-        gate(2, slice(0, T))
+        gate(nc.gpsimd, 1, slice(0, T))
+        gate(nc.gpsimd, 2, slice(0, T))
+        late_scales = keep.tile([P, P], U8, tag=f"in_slot_order1_{HALF}_2", align_bytes=ALIGN)
+        nc.gpsimd.tensor_copy(late_scales[:], w2_scales_by_plane[:, PACK - 1, :])
+        w2_plane_scales.append(late_scales[:])
         for c in range(len(chunks)):
             group_h(c, 0, nc.scalar.copy)
-        turn_and_scatter(1, by_slots, HALF, (3,))
+        turn_and_scatter(1, by_slots_first + by_slots, 0, (3,))
 
-        y_codes = keep.tile([P, T], U32, align_bytes=AL)
-        y_scales = keep.tile([P, T], U8, align_bytes=AL)
-        out_rows = out_0.rearrange("(p d) t -> p d t", d=PACK)
+        unread = psum.tile([P, BANK], F32, tag="sums", bufs=SUM_BANKS)
+        for n in range(WARM_PASSES):
+            nc.tensor.matmul_mx(
+                out=unread[:],
+                lhsT=w2_plane_words[:, PACK - 1, :].bitcast(FP4X4),
+                lhsT_scale=w2_plane_scales[PACK - 1],
+                rhs=later_words[:, 0:T].bitcast(FP8X4),
+                rhs_scale=slot_scales[0][0][:],
+                start=True,
+                stop=True,
+            )
 
-        def second_layer(c, grouped):
-            hq = keep.tile([P, CHUNK], U32, name=f"hq{c}", align_bytes=AL)
-            hs = keep.tile([P, CHUNK], U8, name=f"hs{c}", align_bytes=AL)
-            nc.vector.quantize_mx(out=hq[:].bitcast(FP8X4), scales=hs[:], in_=grouped[:].rearrange("p g t -> p (g t)"))
-            acc = psum.tile([P, PACK, CHUNK], F32, name="turned", bufs=4)
+        y_codes = keep.tile([P, T], U32, align_bytes=ALIGN)
+        y_scales = keep.tile([P, T], U8, align_bytes=ALIGN)
+        out_planes = out_0.rearrange("(p d) t -> p d t", d=PACK)
+
+        def second_product(c):
+            h_codes = keep.tile([P, CHUNK], U32, name=f"h_codes{c}", align_bytes=ALIGN)
+            h_scales = keep.tile([P, CHUNK], U8, name=f"h_scales{c}", align_bytes=ALIGN)
+            nc.vector.quantize_mx(
+                out=h_codes[:].bitcast(FP8X4), scales=h_scales[:], in_=h_grouped[c][:].rearrange("p g t -> p (g t)")
+            )
+            y_sums = psum.tile([P, PACK, CHUNK], F32, tag="turned", bufs=TURN_BANKS)
             for d in range(PACK):
                 nc.tensor.matmul_mx(
-                    out=acc[:, d, :],
-                    lhsT=w2wp[:, d, :].bitcast(FP4X4),
-                    lhsT_scale=w2sp[:, d, :],
-                    rhs=hq[:].bitcast(FP8X4),
-                    rhs_scale=hs[:],
+                    out=y_sums[:, d, :],
+                    lhsT=w2_plane_words[:, d, :].bitcast(FP4X4),
+                    lhsT_scale=w2_plane_scales[d],
+                    rhs=h_codes[:].bitcast(FP8X4),
+                    rhs_scale=h_scales[:],
                     start=True,
                     stop=True,
                 )
-            return acc
+            return y_sums
 
-        def store_y(c, acc):
-            y = keep.tile([P, PACK, CHUNK], F32, name=f"y{c}", align_bytes=AL)
-            nc.scalar.copy(y[:], acc[:])
-            nc.sync.dma_start(out=out_rows[:, :, chunks[c]], in_=y[:])
+        def store_y(c, y_sums):
+            y = keep.tile([P, PACK, CHUNK], F32, name=f"y{c}", align_bytes=ALIGN)
+            nc.scalar.copy(y[:], y_sums[:])
+            nc.sync.dma_start(out=out_planes[:, :, chunks[c]], in_=y[:])
             return y
 
         def quantise_y(c, source):
-            grouped = keep.tile([P, CHUNK, PACK], BF16, name=f"y_grouped{c}", align_bytes=AL)
+            y_grouped = keep.tile([P, CHUNK, PACK], BF16, name=f"y_grouped{c}", align_bytes=ALIGN)
             nc.vector.tensor_copy(
-                grouped[:].rearrange("p (g i) d -> p g d i", i=4), source[:].rearrange("p d (g i) -> p g d i", i=4)
+                y_grouped[:].rearrange("p (g i) d -> p g d i", i=4), source[:].rearrange("p d (g i) -> p g d i", i=4)
             )
             nc.vector.quantize_mx(
                 out=y_codes[:, chunks[c]].bitcast(FP8X4),
                 scales=y_scales[:, chunks[c]],
-                in_=grouped[:].rearrange("p g d -> p (g d)"),
+                in_=y_grouped[:].rearrange("p g d -> p (g d)"),
             )
 
-        gate(PACK - 1, chunks[0])
-        gate(PACK - 1, chunks[1])
-        g0 = group_h(0, 2, nc.vector.tensor_copy)
-        gate(PACK - 1, slice(HALF, T))
-        g1 = group_h(1, 2, nc.scalar.copy)
-        acc0 = second_layer(0, g0)
-        g2 = group_h(2, 2, nc.vector.tensor_copy)
-        g3 = group_h(3, 2, nc.scalar.copy)
-        accs = [acc0, second_layer(1, g1), second_layer(2, g2), second_layer(3, g3)]
-        for c in range(3):
-            quantise_y(c, store_y(c, accs[c]))
-        quantise_y(3, accs[3])
-        store_y(3, accs[3])
-        nc.sync.dma_start(out=out_1[0].rearrange("p t d -> p (t d)").bitcast(I32), in_=y_codes[:].bitcast(I32))
-        for q in range(4):
-            eng = nc.sync if q % 2 else nc.scalar
-            eng.dma_start(out=out_2[0, 4 * q : 4 * q + 4, :].bitcast(I32), in_=y_scales[32 * q : 32 * q + 4, :].bitcast(I32))
+        gate(nc.vector, PACK - 1, chunks[0])
+        gate(nc.vector, PACK - 1, chunks[1])
+        group_h(0, 2, nc.vector.tensor_copy)
+        gate(nc.vector, PACK - 1, slice(HALF, T))
+        group_h(1, 2, nc.scalar.copy)
+        all_sums = [second_product(0)]
+        group_h(2, 2, nc.vector.tensor_copy)
+        group_h(3, 2, nc.scalar.copy)
+        all_sums.extend(second_product(c) for c in range(1, len(chunks)))
+
+        last = len(chunks) - 1
+        for c in range(last):
+            quantise_y(c, store_y(c, all_sums[c]))
+        quantise_y(last, all_sums[last])
+        store_y(last, all_sums[last])
+
+        codes_out = out_1[0].rearrange("p t d -> p (t d)").bitcast(I32)
+        for cols in (slice(0, HALF), slice(HALF, T)):
+            nc.sync.dma_start(out=codes_out[:, cols], in_=y_codes[:, cols].bitcast(I32))
+        for q in range(QUADRANTS):
+            queue = nc.sync if q % 2 else nc.scalar
+            queue.dma_start(out=out_2[0, 4 * q : 4 * q + 4, :].bitcast(I32), in_=y_scales[32 * q : 32 * q + 4, :].bitcast(I32))

@@ -27,7 +27,6 @@ CHUNK = 128
 BANK = 512
 ALIGN = 64
 SUM_BANKS, TURN_BANKS = 3, 4
-WARM_PASSES = 4
 
 
 def tile_moe_pool_silu_kernel(
@@ -37,7 +36,6 @@ def tile_moe_pool_silu_kernel(
     nc = tc.nc
     with ExitStack() as ctx:
         keep = ctx.enter_context(tc.tile_pool(name="keep", bufs=1))
-        ring = ctx.enter_context(tc.tile_pool(name="ring", bufs=1))
         psum = ctx.enter_context(tc.psum_pool(name="psum", bufs=1))
 
         lists = [keep.tile([P, T // 16], U16, name="list_a"), keep.tile([P, T // 16], U16, name="list_b")]
@@ -57,12 +55,13 @@ def tile_moe_pool_silu_kernel(
             for q in range(QUADRANTS):
                 nc.sync.dma_start(out=scales[32 * q : 32 * q + 4].bitcast(I32), in_=rows[4 * q : 4 * q + 4].bitcast(I32))
 
-        def load_pair(w_words, w_scales, pair):
-            pair_words = ring.tile([P, 2 * PASSES, 2 * H], U8, align_bytes=ALIGN)
-            source = w_words[2 * pair : 2 * pair + 2].rearrange("e s p b -> p (e s) b")
-            nc.sync.dma_start(out=pair_words[:].bitcast(I32), in_=source.bitcast(I32))
+        def load_pair_scales(w_scales, pair):
             load_scale_rows(pair_scales, w_scales[2 * pair : 2 * pair + 2].rearrange("e s b i -> b (e s) i"))
-            return pair_words
+
+        def load_words(experts, tag):
+            words = keep.tile([P, experts.shape[0] * PASSES, 2 * H], U8, tag=tag, align_bytes=ALIGN)
+            nc.sync.dma_start(out=words[:].bitcast(I32), in_=experts.rearrange("e s p b -> p (e s) b").bitcast(I32))
+            return words
 
         nc.sync.dma_start(lists[0][:], offs)
         nc.sync.dma_start(lists[1][:], offs2)
@@ -71,7 +70,8 @@ def tile_moe_pool_silu_kernel(
                 out=x_scale_rows[32 * q : 32 * q + 8, 0:T].bitcast(I32), in_=x_scales[:, 4 * q : 4 * q + 4, :].bitcast(I32)
             )
         nc.sync.dma_start(out=x_word_rows[:], in_=x_words.rearrange("s p t d -> p s (t d)").bitcast(I32))
-        pair_words = load_pair(wa_words, wa_scales, 0)
+        wa_pair_words = load_words(wa_words[0:2], "wa_pair_words")
+        load_pair_scales(wa_scales, 0)
 
         def gather_scales(pool):
             both = keep.tile([P, T], U8, name=f"slot_scales{pool}", align_bytes=ALIGN)
@@ -139,33 +139,32 @@ def tile_moe_pool_silu_kernel(
                 nc.vector.tensor_copy(windows[pool][t][:].indirect(offsets), in_slot_order[:, n, :])
 
         for j in range(2):
-            turn_and_scatter(0, [expert(0, 0, j, pair_words)], j * C, (0, 1, 2, 3))
-        pair_words = load_pair(wa_words, wa_scales, 1)
-        by_slots = [expert(0, 1, j, pair_words) for j in range(2)]
-        for planes in ((0, 1), (2, 3)):
-            turn_and_scatter(0, by_slots, HALF, planes)
+            turn_and_scatter(0, [expert(0, 0, j, wa_pair_words)], j * C, (0, 1, 2, 3))
+        load_pair_scales(wa_scales, 1)
+        wa_pair_words = load_words(wa_words[2:4], "wa_pair_words")
+        for j in range(2):
+            turn_and_scatter(0, [expert(0, 1, j, wa_pair_words)], HALF + j * C, (0, 1, 2, 3))
 
-        w2_raw_words = keep.tile([P, 2 * N], U8, tag="first_words0", align_bytes=ALIGN)
-        nc.sync.dma_start(out=w2_raw_words[:].bitcast(I32), in_=w2_words[0].bitcast(I32))
-        w2_raw_scales = keep.tile([P, N], U8, tag="first_words1", align_bytes=ALIGN)
+        wb_all_words = load_words(wb_words, "first_words1")
+        w2_raw_scales = keep.tile([P, N], U8, tag="first_words0", align_bytes=ALIGN)
         nc.gpsimd.memset(w2_raw_scales[:].bitcast(I32), 0)
         load_scale_rows(w2_raw_scales, w2_scales[0])
+        load_pair_scales(wb_scales, 0)
+        w2_raw_words = keep.tile([P, 2 * N], U8, tag="wa_pair_words", align_bytes=ALIGN)
+        nc.sync.dma_start(out=w2_raw_words[:].bitcast(I32), in_=w2_words[0].bitcast(I32))
         w2_plane_words = keep.tile([P, PACK, 2 * P], U8, align_bytes=ALIGN)
         nc.gpsimd.tensor_copy(
             w2_plane_words[:].rearrange("p d (m b) -> p d m b", b=2),
             w2_raw_words[:].rearrange("p (m d b) -> p d m b", d=PACK, b=2),
         )
-        w2_scales_by_plane = w2_raw_scales[:].rearrange("p (m d) -> p d m", d=PACK)
-        early_scales = keep.tile([P, PACK - 1, P], U8, align_bytes=ALIGN)
-        nc.gpsimd.tensor_copy(early_scales[:], w2_scales_by_plane[:, 0 : PACK - 1, :])
-        w2_plane_scales = [early_scales[:, d, :] for d in range(PACK - 1)]
+        w2_plane_scales = keep.tile([P, PACK, P], U8, align_bytes=ALIGN)
+        nc.gpsimd.tensor_copy(w2_plane_scales[:], w2_raw_scales[:].rearrange("p (m d) -> p d m", d=PACK))
 
-        pair_words = load_pair(wb_words, wb_scales, 0)
-        by_slots_first = [expert(1, 0, j, pair_words) for j in range(2)]
+        by_slots_first = [expert(1, 0, j, wb_all_words[:, 0 : 2 * PASSES, :]) for j in range(2)]
         for planes in ((0, 1), (2,)):
             turn_and_scatter(1, by_slots_first, 0, planes)
-        pair_words = load_pair(wb_words, wb_scales, 1)
-        by_slots = [expert(1, 1, j, pair_words) for j in range(2)]
+        load_pair_scales(wb_scales, 1)
+        by_slots = [expert(1, 1, j, wb_all_words[:, 2 * PASSES :, :]) for j in range(2)]
 
         h_planes = keep.tile([P, PACK, T], BF16, align_bytes=ALIGN)
         chunks = [slice(c * CHUNK, (c + 1) * CHUNK) for c in range(T // CHUNK)]
@@ -183,24 +182,9 @@ def tile_moe_pool_silu_kernel(
         turn_and_scatter(1, by_slots, HALF, (2,))
         gate(nc.gpsimd, 1, slice(0, T))
         gate(nc.gpsimd, 2, slice(0, T))
-        late_scales = keep.tile([P, P], U8, tag=f"in_slot_order1_{HALF}_2", align_bytes=ALIGN)
-        nc.gpsimd.tensor_copy(late_scales[:], w2_scales_by_plane[:, PACK - 1, :])
-        w2_plane_scales.append(late_scales[:])
         for c in range(len(chunks)):
             group_h(c, 0, nc.scalar.copy)
         turn_and_scatter(1, by_slots_first + by_slots, 0, (3,))
-
-        unread = psum.tile([P, BANK], F32, tag="sums", bufs=SUM_BANKS)
-        for n in range(WARM_PASSES):
-            nc.tensor.matmul_mx(
-                out=unread[:],
-                lhsT=w2_plane_words[:, PACK - 1, :].bitcast(FP4X4),
-                lhsT_scale=w2_plane_scales[PACK - 1],
-                rhs=later_words[:, 0:T].bitcast(FP8X4),
-                rhs_scale=slot_scales[0][0][:],
-                start=True,
-                stop=True,
-            )
 
         y_codes = keep.tile([P, T], U32, align_bytes=ALIGN)
         y_scales = keep.tile([P, T], U8, align_bytes=ALIGN)
@@ -217,7 +201,7 @@ def tile_moe_pool_silu_kernel(
                 nc.tensor.matmul_mx(
                     out=y_sums[:, d, :],
                     lhsT=w2_plane_words[:, d, :].bitcast(FP4X4),
-                    lhsT_scale=w2_plane_scales[d],
+                    lhsT_scale=w2_plane_scales[:, d, :],
                     rhs=h_codes[:].bitcast(FP8X4),
                     rhs_scale=h_scales[:],
                     start=True,

from contextlib import ExitStack

import concourse.mybir as mybir
from concourse.masks import make_identity

K, T, C, H, N = 1024, 512, 128, 512, 512
FLOPS = 2 * (2 * K * H * T + H * N * T)

F32 = mybir.dt.float32
BF16 = mybir.dt.bfloat16
I32 = mybir.dt.int32
U32 = mybir.dt.uint32
U16 = mybir.dt.uint16
U8 = mybir.dt.uint8
FP8X4 = mybir.dt.float8_e4m3fn_x4
FP4X4 = mybir.dt.float4_e2m1fn_x4
SILU = mybir.ActivationFunctionType.Silu
MULT = mybir.AluOpType.mult

P = 128
PACK = 4
QUADRANTS = 4
PASSES = K // (P * PACK)
HALF = T // 2
WINDOW = 768
CHUNK = 128
BANK = 512
ALIGN = 64
SUM_BANKS, TURN_BANKS = 3, 4


def tile_moe_pool_silu_kernel(
    tc, x_words, x_scales, wa_words, wa_scales, wb_words, wb_scales, w2_words, w2_scales, offs, offs2,
    out_0, out_1, out_2,
):
    nc = tc.nc
    with ExitStack() as ctx:
        keep = ctx.enter_context(tc.tile_pool(name="keep", bufs=1))
        psum = ctx.enter_context(tc.psum_pool(name="psum", bufs=1))

        lists = [keep.tile([P, T // 16], U16, name="list_a"), keep.tile([P, T // 16], U16, name="list_b")]
        x_scale_rows = keep.tile([P, WINDOW], U8, tag="x_scale_rows", align_bytes=ALIGN)
        second_pass_scales = [keep.tile([P, T], U8, name=f"second_pass_scales{pool}", align_bytes=ALIGN) for pool in range(2)]
        x_word_rows = keep.tile([P, PASSES, T], I32, align_bytes=ALIGN)
        pair_scales = keep.tile([P, 2 * PASSES, H], U8, align_bytes=ALIGN)
        identity = keep.tile([P, P], F32, align_bytes=ALIGN)

        nc.gpsimd.memset(x_scale_rows[:].bitcast(I32), 0)
        nc.vector.memset(pair_scales[:].bitcast(I32), 0)
        for scales in second_pass_scales:
            nc.vector.memset(scales[:].bitcast(I32), 0)
        make_identity(nc, identity[:])

        def load_scale_rows(scales, rows):
            for q in range(QUADRANTS):
                nc.sync.dma_start(out=scales[32 * q : 32 * q + 4].bitcast(I32), in_=rows[4 * q : 4 * q + 4].bitcast(I32))

        def load_pair_scales(w_scales, pair):
            load_scale_rows(pair_scales, w_scales[2 * pair : 2 * pair + 2].rearrange("e s b i -> b (e s) i"))

        def load_words(experts, tag):
            words = keep.tile([P, experts.shape[0] * PASSES, 2 * H], U8, tag=tag, align_bytes=ALIGN)
            nc.sync.dma_start(out=words[:].bitcast(I32), in_=experts.rearrange("e s p b -> p (e s) b").bitcast(I32))
            return words

        nc.sync.dma_start(lists[0][:], offs)
        nc.sync.dma_start(lists[1][:], offs2)
        for q in range(QUADRANTS):
            nc.scalar.dma_start(
                out=x_scale_rows[32 * q : 32 * q + 8, 0:T].bitcast(I32), in_=x_scales[:, 4 * q : 4 * q + 4, :].bitcast(I32)
            )
        nc.sync.dma_start(out=x_word_rows[:], in_=x_words.rearrange("s p t d -> p s (t d)").bitcast(I32))
        wa_pair_words = load_words(wa_words[0:2], "wa_pair_words")
        load_pair_scales(wa_scales, 0)

        def gather_scales(pool):
            both = keep.tile([P, T], U8, name=f"slot_scales{pool}", align_bytes=ALIGN)
            nc.vector.tensor_copy(both[:], x_scale_rows[:].indirect(lists[pool][:]))
            for q in range(QUADRANTS):
                nc.sync.dma_start(
                    out=second_pass_scales[pool][32 * q : 32 * q + 4, :].bitcast(I32),
                    in_=both[32 * q + 4 : 32 * q + 8, :].bitcast(I32),
                )
            return both, second_pass_scales[pool]

        def gather_words(pool, pair, targets):
            offsets = lists[pool][:, pair * (HALF // 16) : (pair + 1) * (HALF // 16)]
            for s in range(PASSES):
                nc.vector.tensor_copy(targets[s], x_word_rows[:, s, :].bitcast(U32).indirect(offsets))
            return targets

        first_words = [keep.tile([P, HALF], U32, name=f"first_words{s}", align_bytes=ALIGN) for s in range(PASSES)]
        first_pair = gather_words(0, 0, [tile[:] for tile in first_words])
        slot_scales = [gather_scales(pool) for pool in range(2)]
        later_words = keep.tile([P, 3 * PASSES * HALF], U32, tag="x_scale_rows", align_bytes=ALIGN)
        later = [later_words[:, n * HALF : (n + 1) * HALF] for n in range(3 * PASSES)]
        slot_words = [
            [first_pair, gather_words(0, 1, later[0:PASSES])],
            [gather_words(1, 0, later[PASSES : 2 * PASSES]), gather_words(1, 1, later[2 * PASSES :])],
        ]

        windows = [
            [keep.tile([P, WINDOW], F32, name=f"window{pool}{t}", align_bytes=ALIGN) for t in range(PACK)] for pool in range(2)
        ]

        def expert(pool, pair, j, words):
            e = 2 * pair + j
            sums = psum.tile([P, BANK], F32, bufs=SUM_BANKS)
            for s in range(PASSES):
                nc.tensor.matmul_mx(
                    out=sums[:],
                    lhsT=slot_words[pool][pair][s][:, j * C : (j + 1) * C].bitcast(FP8X4),
                    lhsT_scale=slot_scales[pool][s][:, e * C : (e + 1) * C],
                    rhs=words[:, j * PASSES + s, :].bitcast(FP4X4),
                    rhs_scale=pair_scales[:, j * PASSES + s, :],
                    start=(s == 0),
                    stop=(s == PASSES - 1),
                )
            by_slot = keep.tile([P, PACK, P], F32, name=f"by_slot{e}", align_bytes=ALIGN)
            by_plane = sums[:].rearrange("u (p t) -> u t p", t=PACK)
            if pool == 0:
                nc.scalar.activation(by_slot[:], by_plane, SILU)
            else:
                nc.scalar.copy(by_slot[:], by_plane)
            return by_slot

        def turn_and_scatter(pool, by_slots, first_slot, planes):
            width = len(by_slots) * C
            turned = psum.tile([P, len(planes), width], F32, tag="turned", bufs=TURN_BANKS)
            for n, t in enumerate(planes):
                for j, by_slot in enumerate(by_slots):
                    nc.tensor.transpose(turned[:, n, j * C : (j + 1) * C], by_slot[:, t, :], identity[:])
            in_slot_order = keep.tile(
                [P, len(planes), width], F32, name=f"in_slot_order{pool}_{first_slot}_{planes[0]}", align_bytes=ALIGN
            )
            nc.scalar.copy(in_slot_order[:], turned[:])
            offsets = lists[pool][:, first_slot // 16 : (first_slot + width) // 16]
            for n, t in enumerate(planes):
                nc.vector.tensor_copy(windows[pool][t][:].indirect(offsets), in_slot_order[:, n, :])

        for j in range(2):
            turn_and_scatter(0, [expert(0, 0, j, wa_pair_words)], j * C, (0, 1, 2, 3))
        load_pair_scales(wa_scales, 1)
        wa_pair_words = load_words(wa_words[2:4], "wa_pair_words")
        for j in range(2):
            turn_and_scatter(0, [expert(0, 1, j, wa_pair_words)], HALF + j * C, (0, 1, 2, 3))

        wb_all_words = load_words(wb_words, "first_words1")
        w2_raw_scales = keep.tile([P, N], U8, tag="first_words0", align_bytes=ALIGN)
        nc.gpsimd.memset(w2_raw_scales[:].bitcast(I32), 0)
        load_scale_rows(w2_raw_scales, w2_scales[0])
        load_pair_scales(wb_scales, 0)
        w2_raw_words = keep.tile([P, 2 * N], U8, tag="wa_pair_words", align_bytes=ALIGN)
        nc.sync.dma_start(out=w2_raw_words[:].bitcast(I32), in_=w2_words[0].bitcast(I32))
        w2_plane_words = keep.tile([P, PACK, 2 * P], U8, align_bytes=ALIGN)
        nc.gpsimd.tensor_copy(
            w2_plane_words[:].rearrange("p d (m b) -> p d m b", b=2),
            w2_raw_words[:].rearrange("p (m d b) -> p d m b", d=PACK, b=2),
        )
        w2_plane_scales = keep.tile([P, PACK, P], U8, align_bytes=ALIGN)
        nc.gpsimd.tensor_copy(w2_plane_scales[:], w2_raw_scales[:].rearrange("p (m d) -> p d m", d=PACK))

        by_slots_first = [expert(1, 0, j, wb_all_words[:, 0 : 2 * PASSES, :]) for j in range(2)]
        for planes in ((0, 1), (2,)):
            turn_and_scatter(1, by_slots_first, 0, planes)
        load_pair_scales(wb_scales, 1)
        by_slots = [expert(1, 1, j, wb_all_words[:, 2 * PASSES :, :]) for j in range(2)]

        h_planes = keep.tile([P, PACK, T], BF16, align_bytes=ALIGN)
        chunks = [slice(c * CHUNK, (c + 1) * CHUNK) for c in range(T // CHUNK)]
        h_grouped = [keep.tile([P, CHUNK, PACK], BF16, name=f"h_grouped{c}", align_bytes=ALIGN) for c in range(len(chunks))]

        def gate(engine, t, cols):
            engine.tensor_tensor(h_planes[:, t, cols], windows[0][t][:, cols], windows[1][t][:, cols], MULT)

        def group_h(c, first_plane, copy):
            two = slice(first_plane, first_plane + 2)
            copy(h_grouped[c][:, :, two], h_planes[:, two, chunks[c]].rearrange("p t g -> p g t"))

        turn_and_scatter(1, by_slots, HALF, (0, 1))
        gate(nc.gpsimd, 0, slice(0, T))
        turn_and_scatter(1, by_slots, HALF, (2,))
        gate(nc.gpsimd, 1, slice(0, T))
        gate(nc.gpsimd, 2, slice(0, T))
        for c in range(len(chunks)):
            group_h(c, 0, nc.scalar.copy)
        turn_and_scatter(1, by_slots_first + by_slots, 0, (3,))

        y_codes = keep.tile([P, T], U32, align_bytes=ALIGN)
        y_scales = keep.tile([P, T], U8, align_bytes=ALIGN)
        out_planes = out_0.rearrange("(p d) t -> p d t", d=PACK)

        def second_product(c):
            h_codes = keep.tile([P, CHUNK], U32, name=f"h_codes{c}", align_bytes=ALIGN)
            h_scales = keep.tile([P, CHUNK], U8, name=f"h_scales{c}", align_bytes=ALIGN)
            nc.vector.quantize_mx(
                out=h_codes[:].bitcast(FP8X4), scales=h_scales[:], in_=h_grouped[c][:].rearrange("p g t -> p (g t)")
            )
            y_sums = psum.tile([P, PACK, CHUNK], F32, tag="turned", bufs=TURN_BANKS)
            for d in range(PACK):
                nc.tensor.matmul_mx(
                    out=y_sums[:, d, :],
                    lhsT=w2_plane_words[:, d, :].bitcast(FP4X4),
                    lhsT_scale=w2_plane_scales[:, d, :],
                    rhs=h_codes[:].bitcast(FP8X4),
                    rhs_scale=h_scales[:],
                    start=True,
                    stop=True,
                )
            return y_sums

        def store_y(c, y_sums):
            y = keep.tile([P, PACK, CHUNK], F32, name=f"y{c}", align_bytes=ALIGN)
            nc.scalar.copy(y[:], y_sums[:])
            nc.sync.dma_start(out=out_planes[:, :, chunks[c]], in_=y[:])
            return y

        def quantise_y(c, source):
            y_grouped = keep.tile([P, CHUNK, PACK], BF16, name=f"y_grouped{c}", align_bytes=ALIGN)
            nc.vector.tensor_copy(
                y_grouped[:].rearrange("p (g i) d -> p g d i", i=4), source[:].rearrange("p d (g i) -> p g d i", i=4)
            )
            nc.vector.quantize_mx(
                out=y_codes[:, chunks[c]].bitcast(FP8X4),
                scales=y_scales[:, chunks[c]],
                in_=y_grouped[:].rearrange("p g d -> p (g d)"),
            )

        gate(nc.vector, PACK - 1, chunks[0])
        gate(nc.vector, PACK - 1, chunks[1])
        group_h(0, 2, nc.vector.tensor_copy)
        gate(nc.vector, PACK - 1, slice(HALF, T))
        group_h(1, 2, nc.scalar.copy)
        all_sums = [second_product(0)]
        group_h(2, 2, nc.vector.tensor_copy)
        group_h(3, 2, nc.scalar.copy)
        all_sums.extend(second_product(c) for c in range(1, len(chunks)))

        last = len(chunks) - 1
        for c in range(last):
            quantise_y(c, store_y(c, all_sums[c]))
        quantise_y(last, all_sums[last])
        store_y(last, all_sums[last])

        codes_out = out_1[0].rearrange("p t d -> p (t d)").bitcast(I32)
        for cols in (slice(0, HALF), slice(HALF, T)):
            nc.sync.dma_start(out=codes_out[:, cols], in_=y_codes[:, cols].bitcast(I32))
        for q in range(QUADRANTS):
            queue = nc.sync if q % 2 else nc.scalar
            queue.dma_start(out=out_2[0, 4 * q : 4 * q + 4, :].bitcast(I32), in_=y_scales[32 * q : 32 * q + 4, :].bitcast(I32))
